import numpy as np
import ml_dtypes


def mxq(x, axis, fmt="e4m3"):
    dtype, down = {"e4m3": (ml_dtypes.float8_e4m3fn, 7), "e5m2": (ml_dtypes.float8_e5m2, 14)}[fmt]
    v = np.moveaxis(np.asarray(x, np.float32).astype(ml_dtypes.bfloat16).astype(np.float64), axis, -1)
    blocks = v.reshape(v.shape[:-1] + (-1, 32))
    amax = np.abs(blocks).max(-1, keepdims=True)
    byte = np.maximum(np.where(amax > 0, np.frexp(amax)[1] - 1 + 127, 0) - down, 1)
    scale = np.exp2(byte - 127.0)
    codes = (blocks / scale).astype(np.float32).astype(dtype).astype(np.float64)
    return np.moveaxis((codes * scale).reshape(v.shape), -1, axis)


WIDE = False


def mx_kscale(k):
    if not WIDE:
        return np.ones(k)
    levels = np.array([10, -10, 5, -5, 0])
    if k % 512:
        return np.exp2(np.random.permutation(np.resize(levels, k // 32))).repeat(32)
    a = np.empty((k // 512, 16))
    for p in range(k // 512):
        a[p, :8] = np.random.permutation(np.resize(levels, 8))
        for g in range(8):
            far = levels[np.abs(levels - a[p, g]) >= 10]
            a[p, g + 8] = far[np.random.randint(len(far))]
    return np.exp2(a.ravel()).repeat(32)


def f64(x):
    return np.asarray(x).astype(np.float64)


def striped(idx):
    return np.tile(idx.reshape(-1, 16).T, (8, 1)).astype(np.uint16)


def unstriped(offs):
    return offs[:16].T.reshape(-1).astype(np.int64)


E2M1 = np.array([0.0, 0.5, 1.0, 1.5, 2.0, 3.0, 4.0, 6.0, -0.0, -0.5, -1.0, -1.5, -2.0, -3.0, -4.0, -6.0])


def pack_weight(w, fmt):
    k, n = w.shape
    w = f64(np.asarray(w, np.float32).astype(ml_dtypes.bfloat16)).reshape(k // 32, 32, n)
    amax = np.abs(w).max(1)
    if fmt == "e4m3":
        byte = np.frexp(amax)[1] - 1 + 127 - 7
    else:
        mant, ex = np.frexp(amax / 6.0)
        byte = np.where(mant > 0.5, ex, ex - 1) + 127
    byte = np.clip(np.where(amax > 0, byte, 1), 1, 254)
    scaled = (w * np.exp2(127.0 - byte)[:, None, :]).reshape(k, n).astype(np.float32)
    by_word = np.ascontiguousarray(scaled.reshape(k // 512, 128, 4, n).transpose(0, 1, 3, 2))
    if fmt == "e4m3":
        words = by_word.astype(ml_dtypes.float8_e4m3fn).view(np.uint8)
    else:
        c = by_word.astype(ml_dtypes.float4_e2m1fn).view(np.uint8) & 0xF
        words = (c[..., 0::2] | (c[..., 1::2] << 4)).reshape(k // 512, 128, 2 * n)
    return np.ascontiguousarray(words), np.ascontiguousarray(byte.astype(np.uint8).reshape(k // 512, 16, n))


def unpack_weight(words, scales, fmt):
    g, _, n = scales.shape
    words = np.ascontiguousarray(words).reshape(g, 128, n, -1)
    if fmt == "e4m3":
        vals = words.view(ml_dtypes.float8_e4m3fn).astype(np.float64)
    else:
        nib = np.empty((g, 128, n, 4), np.uint8)
        nib[..., 0::2] = words & 0xF
        nib[..., 1::2] = words >> 4
        vals = E2M1[nib]
    vals = vals * np.repeat(np.exp2(scales.astype(np.float64) - 127.0), 8, axis=1)[..., None]
    return vals.transpose(0, 1, 3, 2).reshape(g * 512, n)


def relu2(v):
    return np.maximum(v, 0.0) ** 2


K, T, E, N = 512, 4096, 8, 128
COUNTS = (128, 128, 512, 640, 896, 896, 384, 512)
STARTS = np.cumsum((0,) + COUNTS)


def by_expert(wq, xq):
    return np.concatenate([wq[e].T @ xq[:, STARTS[e]:STARTS[e + 1]] for e in range(E)], axis=1)


def setup_inputs():
    n = np.random.standard_normal
    s = mx_kscale(K)[:, None]
    expert = np.random.permutation(np.repeat(np.arange(E), COUNTS))
    slot_token = np.argsort(expert, kind="stable")
    w = [pack_weight(m, "e2m1") for m in n((E, K, N)) / np.sqrt(K) / s[None]]
    return {
        "xT": (n((K, T)) * s).astype(np.float32),
        "w_words": np.stack([m[0] for m in w]),
        "w_scales": np.stack([m[1] for m in w]),
        "b": (0.3 * n((N, E))).astype(np.float32),
        "gate": np.tile(np.random.uniform(0.2, 1.0, T), (N, 1)).astype(np.float32),
        "offs": striped(slot_token),
    }


def reference(xT, w_words, w_scales, b, gate, offs):
    idx = unstriped(offs)
    w = np.stack([unpack_weight(w_words[e], w_scales[e], "e2m1") for e in range(E)])
    xq = mxq(f64(xT)[:, idx], 0, "e4m3")
    y = by_expert(w, xq)
    y = relu2(y + np.repeat(f64(b), COUNTS, axis=1))
    out = np.zeros((N, T))
    out[:, idx] = f64(gate) * y
    return out

@@ -1,0 +1,173 @@
+import concourse.mybir as mybir
+
+F32 = mybir.dt.float32
+BF16 = mybir.dt.bfloat16
+U32 = mybir.dt.uint32
+I32 = mybir.dt.int32
+U16 = mybir.dt.uint16
+U8 = mybir.dt.uint8
+FP8X4 = mybir.dt.float8_e4m3fn_x4
+FP4X4 = mybir.dt.float4_e2m1fn_x4
+RELU = mybir.ActivationFunctionType.Relu
+SQUARE = mybir.ActivationFunctionType.Square
+MULT = mybir.AluOpType.mult
+
+P, T, E, N, K = 128, 4096, 8, 128, 512
+COUNTS = (128, 128, 512, 640, 896, 896, 384, 512)
+FLOPS = 2 * K * N * T
+CH = 512
+NCH = T // CH
+V_LACE = (0, 1, 4)
+
+
+def pieces_of(c):
+    found = []
+    start = 0
+    for e in range(E):
+        lo, hi = max(start, c * CH), min(start + COUNTS[e], (c + 1) * CH)
+        start += COUNTS[e]
+        while lo < hi:
+            width = max(n for n in (128, 256, 512) if n <= hi - lo)
+            found.append((lo - c * CH, width, e))
+            lo += width
+    return found
+
+
+def spans_of(c):
+    found = []
+    start = 0
+    for e in range(E):
+        lo, hi = max(start, c * CH), min(start + COUNTS[e], (c + 1) * CH)
+        start += COUNTS[e]
+        if lo < hi:
+            found.append((lo - c * CH, hi - c * CH, e))
+    return found
+
+
+def tile_moe_rag_lin_relu2_kernel(tc, xT, w_words, w_scales, b, gate, offs, out):
+    nc = tc.nc
+    with (
+        tc.tile_pool(name="held", bufs=1) as held,
+        tc.tile_pool(name="ring", bufs=3) as ring,
+        tc.psum_pool(name="psum", bufs=4) as psum,
+    ):
+        offsets = held.tile([P, T // 16], U16, name="offsets")
+        nc.sync.dma_start(offsets[:], offs)
+
+        w_sb = held.tile([P, E, 2 * N], U8, name="w_sb", align_bytes=64)
+        ws_sb = held.tile([P, E, N], U8, name="ws_sb", align_bytes=64)
+        b_sb = held.tile([P, E], F32, name="b_sb")
+        nc.vector.memset(ws_sb[:].rearrange("p e n -> p (e n)").bitcast(I32), 0)
+        for q in range(4):
+            nc.gpsimd.dma_start(
+                out=ws_sb[32 * q : 32 * q + 4].bitcast(I32),
+                in_=w_scales[:, 0, 4 * q : 4 * q + 4, :].rearrange("e q n -> q e n").bitcast(I32),
+            )
+        nc.gpsimd.dma_start(out=b_sb[:], in_=b)
+
+        rows = xT.rearrange("(p j) n -> p j n", j=4)
+        loads = []
+        for h, cuts in ((0, (0, 1024, 2048, 3072, 4096)), (1, (0, 1024, 2048, 3072, 3584, 4096))):
+            for lo, hi in zip(cuts[:-1], cuts[1:]):
+                raw = held.tile([P, 2, hi - lo], F32, name="raw" + str(h) + "_" + str(lo))
+                nc.sync.dma_start(out=raw[:], in_=rows[:, 2 * h : 2 * h + 2, lo:hi])
+                loads.append((h, lo, hi, raw))
+        nc.sync.dma_start(
+            out=w_sb[:].bitcast(I32), in_=w_words[:, 0].rearrange("e p n -> p e n").bitcast(I32)
+        )
+        gate_sb = held.tile([P, T], F32, name="gate_sb")
+        for lo in range(0, T, 1024):
+            nc.sync.dma_start(out=gate_sb[:, lo : lo + 1024], in_=gate[:, lo : lo + 1024])
+
+        pairs = [held.tile([P, T, 2], BF16, name="pairs" + str(h), align_bytes=64) for h in (0, 1)]
+        window = [t[:].rearrange("p n e -> p (n e)").bitcast(U32) for t in pairs]
+        mates = [held.tile([P, 2, 2 * CH, 2], BF16, name="mates" + str(i), align_bytes=64) for i in range(NCH // 2)]
+        result = held.tile([P, T], F32, name="result")
+
+        def cast(load, v_cols):
+            h, lo, hi, raw = load
+            if v_cols:
+                nc.vector.tensor_copy(
+                    out=pairs[h][:, lo : lo + v_cols, :], in_=raw[:, :, 0:v_cols].rearrange("p e n -> p n e")
+                )
+            if lo + v_cols < hi:
+                nc.scalar.copy(
+                    out=pairs[h][:, lo + v_cols : hi, :], in_=raw[:, :, v_cols : hi - lo].rearrange("p e n -> p n e")
+                )
+
+        def gather(h, lo, hi):
+            i, at = lo // (2 * CH), lo % (2 * CH)
+            nc.vector.tensor_copy(
+                out=mates[i][:, h, at : at + hi - lo, :].rearrange("p n e -> p (n e)").bitcast(U32),
+                in_=window[h].indirect(offsets[:, lo // 16 : hi // 16]),
+            )
+
+        laced = {}
+        codes = {}
+        squares = {}
+
+        def lace(c):
+            i, at = c // 2, (c % 2) * CH
+            x4 = ring.tile([P, CH, 2, 2], BF16, name="x4", align_bytes=64)
+            src = mates[i][:, :, at : at + CH, :].rearrange("p h n e -> p n h e")
+            if c in V_LACE:
+                nc.vector.tensor_copy(out=x4[:], in_=src)
+            else:
+                nc.scalar.copy(out=x4[:], in_=src)
+            laced[c] = x4
+
+        def quantise(c):
+            cw = ring.tile([P, CH], U32, name="cw", align_bytes=64)
+            cs = ring.tile([P, CH], U8, name="cs", align_bytes=64)
+            nc.vector.quantize_mx(
+                out=cw[:].bitcast(FP8X4), scales=cs[:], in_=laced[c][:].rearrange("p n h e -> p (n h e)")
+            )
+            codes[c] = (cw, cs)
+
+        def multiply(c):
+            cw, cs = codes[c]
+            bank = psum.tile([N, CH], F32, name="bank")
+            for at, width, e in pieces_of(c):
+                nc.tensor.matmul_mx(
+                    out=bank[:, at : at + width],
+                    lhsT=w_sb[:, e, :].bitcast(FP4X4),
+                    lhsT_scale=ws_sb[:, e, :],
+                    rhs=cw[:, at : at + width].bitcast(FP8X4),
+                    rhs_scale=cs[:, at : at + width],
+                    start=True,
+                    stop=True,
+                )
+            relu = ring.tile([N, CH], F32, name="relu")
+            for lo, hi, e in spans_of(c):
+                nc.scalar.activation(relu[:, lo:hi], bank[:, lo:hi], RELU, bias=b_sb[:, e : e + 1])
+            square = ring.tile([N, CH], F32, name="square")
+            nc.scalar.activation(square[:], relu[:], SQUARE)
+            squares[c] = square
+
+        def scatter(c):
+            cols = slice(c * CH, (c + 1) * CH)
+            nc.vector.tensor_tensor(
+                result[:].indirect(offsets[:, c * CH // 16 : (c + 1) * CH // 16]), squares[c][:], gate_sb[:, cols], MULT
+            )
+
+        for load in loads[0:3]:
+            cast(load, 1024)
+        cast(loads[3], 640)
+        for i in range(4):
+            gather(0, 1024 * i, 1024 * (i + 1))
+            cast(loads[4 + i], (256, 256, 256, 192)[i])
+        cast(loads[8], 256)
+
+        for step in range(NCH + 4):
+            if step < NCH:
+                gather(1, step * CH, (step + 1) * CH)
+            if 0 <= step - 1 < NCH:
+                lace(step - 1)
+            if 0 <= step - 2 < NCH:
+                quantise(step - 2)
+                multiply(step - 2)
+            if 0 <= step - 4 < NCH:
+                scatter(step - 4)
+        for i, lo in enumerate(range(0, T, 1024)):
+            queue = (nc.sync, nc.scalar)[i % 2]
+            queue.dma_start(out=out[:, lo : lo + 1024], in_=result[:, lo : lo + 1024])

@@ -11,13 +11,14 @@ FP4X4 = mybir.dt.float4_e2m1fn_x4
 RELU = mybir.ActivationFunctionType.Relu
 SQUARE = mybir.ActivationFunctionType.Square
 MULT = mybir.AluOpType.mult
+ADD = mybir.AluOpType.add
 
 P, T, E, N, K = 128, 4096, 8, 128, 512
 COUNTS = (128, 128, 512, 640, 896, 896, 384, 512)
 FLOPS = 2 * K * N * T
 CH = 512
 NCH = T // CH
-V_LACE = (0, 1, 4)
+V_LACE = (0,)
 
 
 def pieces_of(c):
@@ -59,15 +60,15 @@ def tile_moe_rag_lin_relu2_kernel(tc, xT, w_words, w_scales, b, gate, offs, out)
         b_sb = held.tile([P, E], F32, name="b_sb")
         nc.vector.memset(ws_sb[:].rearrange("p e n -> p (e n)").bitcast(I32), 0)
         for q in range(4):
-            nc.gpsimd.dma_start(
+            nc.scalar.dma_start(
                 out=ws_sb[32 * q : 32 * q + 4].bitcast(I32),
                 in_=w_scales[:, 0, 4 * q : 4 * q + 4, :].rearrange("e q n -> q e n").bitcast(I32),
             )
-        nc.gpsimd.dma_start(out=b_sb[:], in_=b)
+        nc.scalar.dma_start(out=b_sb[:], in_=b)
 
         rows = xT.rearrange("(p j) n -> p j n", j=4)
         loads = []
-        for h, cuts in ((0, (0, 1024, 2048, 3072, 4096)), (1, (0, 1024, 2048, 3072, 3584, 4096))):
+        for h, cuts in ((0, (0, 1024, 2048, 3072, 3584, 4096)), (1, (0, 1024, 2048, 3072, 3584, 4096))):
             for lo, hi in zip(cuts[:-1], cuts[1:]):
                 raw = held.tile([P, 2, hi - lo], F32, name="raw" + str(h) + "_" + str(lo))
                 nc.sync.dma_start(out=raw[:], in_=rows[:, 2 * h : 2 * h + 2, lo:hi])
@@ -81,22 +82,26 @@ def tile_moe_rag_lin_relu2_kernel(tc, xT, w_words, w_scales, b, gate, offs, out)
 
         pairs = [held.tile([P, T, 2], BF16, name="pairs" + str(h), align_bytes=64) for h in (0, 1)]
         window = [t[:].rearrange("p n e -> p (n e)").bitcast(U32) for t in pairs]
-        mates = [held.tile([P, 2, 2 * CH, 2], BF16, name="mates" + str(i), align_bytes=64) for i in range(NCH // 2)]
+        mates = [held.tile([P, 2, 4 * CH, 2], BF16, name="mates" + str(i), align_bytes=64) for i in range(NCH // 4)]
         result = held.tile([P, T], F32, name="result")
 
-        def cast(load, v_cols):
+        def cast(load, cuts):
             h, lo, hi, raw = load
-            if v_cols:
-                nc.vector.tensor_copy(
-                    out=pairs[h][:, lo : lo + v_cols, :], in_=raw[:, :, 0:v_cols].rearrange("p e n -> p n e")
-                )
-            if lo + v_cols < hi:
-                nc.scalar.copy(
-                    out=pairs[h][:, lo + v_cols : hi, :], in_=raw[:, :, v_cols : hi - lo].rearrange("p e n -> p n e")
-                )
+            bounds = (0,) + cuts + (hi - lo,)
+            for i in range(3):
+                a, z = bounds[i], bounds[i + 1]
+                if a < z:
+                    dst = pairs[h][:, lo + a : lo + z, :]
+                    src = raw[:, :, a:z].rearrange("p e n -> p n e")
+                    if i == 0:
+                        nc.vector.tensor_copy(out=dst, in_=src)
+                    elif i == 1:
+                        nc.scalar.copy(out=dst, in_=src)
+                    else:
+                        nc.gpsimd.tensor_scalar(dst, src, 1.0, 0.0, MULT, ADD)
 
         def gather(h, lo, hi):
-            i, at = lo // (2 * CH), lo % (2 * CH)
+            i, at = lo // (4 * CH), lo % (4 * CH)
             nc.vector.tensor_copy(
                 out=mates[i][:, h, at : at + hi - lo, :].rearrange("p n e -> p (n e)").bitcast(U32),
                 in_=window[h].indirect(offsets[:, lo // 16 : hi // 16]),
@@ -107,7 +112,7 @@ def tile_moe_rag_lin_relu2_kernel(tc, xT, w_words, w_scales, b, gate, offs, out)
         squares = {}
 
         def lace(c):
-            i, at = c // 2, (c % 2) * CH
+            i, at = c // 4, (c % 4) * CH
             x4 = ring.tile([P, CH, 2, 2], BF16, name="x4", align_bytes=64)
             src = mates[i][:, :, at : at + CH, :].rearrange("p h n e -> p n h e")
             if c in V_LACE:
@@ -151,12 +156,15 @@ def tile_moe_rag_lin_relu2_kernel(tc, xT, w_words, w_scales, b, gate, offs, out)
             )
 
         for load in loads[0:3]:
-            cast(load, 1024)
-        cast(loads[3], 640)
-        for i in range(4):
-            gather(0, 1024 * i, 1024 * (i + 1))
-            cast(loads[4 + i], (256, 256, 256, 192)[i])
-        cast(loads[8], 256)
+            cast(load, (1024, 1024))
+        for load in loads[3:5]:
+            cast(load, (320, 512))
+        for load in loads[5:8]:
+            cast(load, (0, 768))
+        cast(loads[8], (0, 384))
+        gather(0, 0, 2048)
+        gather(0, 2048, 4096)
+        cast(loads[9], (64, 320))
 
         for step in range(NCH + 4):
             if step < NCH:

@@ -68,7 +68,7 @@ def tile_moe_rag_lin_relu2_kernel(tc, xT, w_words, w_scales, b, gate, offs, out)
 
         rows = xT.rearrange("(p j) n -> p j n", j=4)
         loads = []
-        for h, cuts in ((0, (0, 1024, 2048, 3072, 3584, 4096)), (1, (0, 1024, 2048, 3072, 3584, 4096))):
+        for h, cuts in ((0, (0, 2048, 3072, 3584, 4096)), (1, (0, 1024, 2048, 3072, 3584, 4096))):
             for lo, hi in zip(cuts[:-1], cuts[1:]):
                 raw = held.tile([P, 2, hi - lo], F32, name="raw" + str(h) + "_" + str(lo))
                 nc.sync.dma_start(out=raw[:], in_=rows[:, 2 * h : 2 * h + 2, lo:hi])
@@ -155,20 +155,22 @@ def tile_moe_rag_lin_relu2_kernel(tc, xT, w_words, w_scales, b, gate, offs, out)
                 result[:].indirect(offsets[:, c * CH // 16 : (c + 1) * CH // 16]), squares[c][:], gate_sb[:, cols], MULT
             )
 
-        for load in loads[0:3]:
-            cast(load, (1024, 1024))
-        for load in loads[3:5]:
+        cast(loads[0], (1280, 2048))
+        cast(loads[1], (704, 1024))
+        for load in loads[2:4]:
             cast(load, (320, 512))
-        for load in loads[5:8]:
+        for load in loads[4:7]:
             cast(load, (0, 768))
-        cast(loads[8], (0, 384))
+        cast(loads[7], (0, 384))
         gather(0, 0, 2048)
         gather(0, 2048, 4096)
-        cast(loads[9], (64, 320))
+        cast(loads[8], (160, 384))
 
         for step in range(NCH + 4):
-            if step < NCH:
+            if step in (0, 1):
                 gather(1, step * CH, (step + 1) * CH)
+            if step in (2, 4, 6):
+                gather(1, step * CH, (step + 2) * CH)
             if 0 <= step - 1 < NCH:
                 lace(step - 1)
             if 0 <= step - 2 < NCH:
@@ -176,6 +178,5 @@ def tile_moe_rag_lin_relu2_kernel(tc, xT, w_words, w_scales, b, gate, offs, out)
                 multiply(step - 2)
             if 0 <= step - 4 < NCH:
                 scatter(step - 4)
-        for i, lo in enumerate(range(0, T, 1024)):
-            queue = (nc.sync, nc.scalar)[i % 2]
-            queue.dma_start(out=out[:, lo : lo + 1024], in_=result[:, lo : lo + 1024])
+        for queue, lo in ((nc.sync, 0), (nc.scalar, 2048)):
+            queue.dma_start(out=out[:, lo : lo + 2048], in_=result[:, lo : lo + 2048])

@@ -59,12 +59,6 @@ def tile_moe_rag_lin_relu2_kernel(tc, xT, w_words, w_scales, b, gate, offs, out)
         ws_sb = held.tile([P, E, N], U8, name="ws_sb", align_bytes=64)
         b_sb = held.tile([P, E], F32, name="b_sb")
         nc.vector.memset(ws_sb[:].rearrange("p e n -> p (e n)").bitcast(I32), 0)
-        for q in range(4):
-            nc.scalar.dma_start(
-                out=ws_sb[32 * q : 32 * q + 4].bitcast(I32),
-                in_=w_scales[:, 0, 4 * q : 4 * q + 4, :].rearrange("e q n -> q e n").bitcast(I32),
-            )
-        nc.scalar.dma_start(out=b_sb[:], in_=b)
 
         rows = xT.rearrange("(p j) n -> p j n", j=4)
         loads = []
@@ -73,6 +67,13 @@ def tile_moe_rag_lin_relu2_kernel(tc, xT, w_words, w_scales, b, gate, offs, out)
                 raw = held.tile([P, 2, hi - lo], F32, name="raw" + str(h) + "_" + str(lo))
                 nc.sync.dma_start(out=raw[:], in_=rows[:, 2 * h : 2 * h + 2, lo:hi])
                 loads.append((h, lo, hi, raw))
+            if h == 0:
+                for q in range(4):
+                    nc.sync.dma_start(
+                        out=ws_sb[32 * q : 32 * q + 4].bitcast(I32),
+                        in_=w_scales[:, 0, 4 * q : 4 * q + 4, :].rearrange("e q n -> q e n").bitcast(I32),
+                    )
+                nc.sync.dma_start(out=b_sb[:], in_=b)
         nc.sync.dma_start(
             out=w_sb[:].bitcast(I32), in_=w_words[:, 0].rearrange("e p n -> p e n").bitcast(I32)
         )
@@ -159,9 +160,10 @@ def tile_moe_rag_lin_relu2_kernel(tc, xT, w_words, w_scales, b, gate, offs, out)
         cast(loads[1], (704, 1024))
         for load in loads[2:4]:
             cast(load, (320, 512))
-        for load in loads[4:7]:
+        for load in loads[4:6]:
             cast(load, (0, 768))
-        cast(loads[7], (0, 384))
+        cast(loads[6], (0, 640))
+        cast(loads[7], (0, 288))
         gather(0, 0, 2048)
         gather(0, 2048, 4096)
         cast(loads[8], (160, 384))

import concourse.mybir as mybir

F32 = mybir.dt.float32
BF16 = mybir.dt.bfloat16
U32 = mybir.dt.uint32
I32 = mybir.dt.int32
U16 = mybir.dt.uint16
U8 = mybir.dt.uint8
FP8X4 = mybir.dt.float8_e4m3fn_x4
FP4X4 = mybir.dt.float4_e2m1fn_x4
RELU = mybir.ActivationFunctionType.Relu
SQUARE = mybir.ActivationFunctionType.Square
MULT = mybir.AluOpType.mult
ADD = mybir.AluOpType.add

P, T, E, N, K = 128, 4096, 8, 128, 512
COUNTS = (128, 128, 512, 640, 896, 896, 384, 512)
FLOPS = 2 * K * N * T
CH = 512
NCH = T // CH
V_LACE = (0,)


def pieces_of(c):
    found = []
    start = 0
    for e in range(E):
        lo, hi = max(start, c * CH), min(start + COUNTS[e], (c + 1) * CH)
        start += COUNTS[e]
        while lo < hi:
            width = max(n for n in (128, 256, 512) if n <= hi - lo)
            found.append((lo - c * CH, width, e))
            lo += width
    return found


def spans_of(c):
    found = []
    start = 0
    for e in range(E):
        lo, hi = max(start, c * CH), min(start + COUNTS[e], (c + 1) * CH)
        start += COUNTS[e]
        if lo < hi:
            found.append((lo - c * CH, hi - c * CH, e))
    return found


def tile_moe_rag_lin_relu2_kernel(tc, xT, w_words, w_scales, b, gate, offs, out):
    nc = tc.nc
    with (
        tc.tile_pool(name="held", bufs=1) as held,
        tc.tile_pool(name="ring", bufs=3) as ring,
        tc.psum_pool(name="psum", bufs=4) as psum,
    ):
        offsets = held.tile([P, T // 16], U16, name="offsets")
        nc.sync.dma_start(offsets[:], offs)

        w_sb = held.tile([P, E, 2 * N], U8, name="w_sb", align_bytes=64)
        ws_sb = held.tile([P, E, N], U8, name="ws_sb", align_bytes=64)
        b_sb = held.tile([P, E], F32, name="b_sb")
        nc.vector.memset(ws_sb[:].rearrange("p e n -> p (e n)").bitcast(I32), 0)

        rows = xT.rearrange("(p j) n -> p j n", j=4)
        loads = []
        for h, cuts in ((0, (0, 2048, 3072, 3584, 4096)), (1, (0, 1024, 2048, 3072, 3584, 4096))):
            for lo, hi in zip(cuts[:-1], cuts[1:]):
                raw = held.tile([P, 2, hi - lo], F32, name="raw" + str(h) + "_" + str(lo))
                nc.sync.dma_start(out=raw[:], in_=rows[:, 2 * h : 2 * h + 2, lo:hi])
                loads.append((h, lo, hi, raw))
            if h == 0:
                for q in range(4):
                    nc.sync.dma_start(
                        out=ws_sb[32 * q : 32 * q + 4].bitcast(I32),
                        in_=w_scales[:, 0, 4 * q : 4 * q + 4, :].rearrange("e q n -> q e n").bitcast(I32),
                    )
                nc.sync.dma_start(out=b_sb[:], in_=b)
        nc.sync.dma_start(
            out=w_sb[:].bitcast(I32), in_=w_words[:, 0].rearrange("e p n -> p e n").bitcast(I32)
        )
        gate_sb = held.tile([P, T], F32, name="gate_sb")
        for lo in range(0, T, 1024):
            nc.sync.dma_start(out=gate_sb[:, lo : lo + 1024], in_=gate[:, lo : lo + 1024])

        pairs = [held.tile([P, T, 2], BF16, name="pairs" + str(h), align_bytes=64) for h in (0, 1)]
        window = [t[:].rearrange("p n e -> p (n e)").bitcast(U32) for t in pairs]
        mates = [held.tile([P, 2, 4 * CH, 2], BF16, name="mates" + str(i), align_bytes=64) for i in range(NCH // 4)]
        result = held.tile([P, T], F32, name="result")

        def cast(load, cuts):
            h, lo, hi, raw = load
            bounds = (0,) + cuts + (hi - lo,)
            for i in range(3):
                a, z = bounds[i], bounds[i + 1]
                if a < z:
                    dst = pairs[h][:, lo + a : lo + z, :]
                    src = raw[:, :, a:z].rearrange("p e n -> p n e")
                    if i == 0:
                        nc.vector.tensor_copy(out=dst, in_=src)
                    elif i == 1:
                        nc.scalar.copy(out=dst, in_=src)
                    else:
                        nc.gpsimd.tensor_scalar(dst, src, 1.0, 0.0, MULT, ADD)

        def gather(h, lo, hi):
            i, at = lo // (4 * CH), lo % (4 * CH)
            nc.vector.tensor_copy(
                out=mates[i][:, h, at : at + hi - lo, :].rearrange("p n e -> p (n e)").bitcast(U32),
                in_=window[h].indirect(offsets[:, lo // 16 : hi // 16]),
            )

        laced = {}
        codes = {}
        squares = {}

        def lace(c):
            i, at = c // 4, (c % 4) * CH
            x4 = ring.tile([P, CH, 2, 2], BF16, name="x4", align_bytes=64)
            src = mates[i][:, :, at : at + CH, :].rearrange("p h n e -> p n h e")
            if c in V_LACE:
                nc.vector.tensor_copy(out=x4[:], in_=src)
            else:
                nc.scalar.copy(out=x4[:], in_=src)
            laced[c] = x4

        def quantise(c):
            cw = ring.tile([P, CH], U32, name="cw", align_bytes=64)
            cs = ring.tile([P, CH], U8, name="cs", align_bytes=64)
            nc.vector.quantize_mx(
                out=cw[:].bitcast(FP8X4), scales=cs[:], in_=laced[c][:].rearrange("p n h e -> p (n h e)")
            )
            codes[c] = (cw, cs)

        def multiply(c):
            cw, cs = codes[c]
            bank = psum.tile([N, CH], F32, name="bank")
            for at, width, e in pieces_of(c):
                nc.tensor.matmul_mx(
                    out=bank[:, at : at + width],
                    lhsT=w_sb[:, e, :].bitcast(FP4X4),
                    lhsT_scale=ws_sb[:, e, :],
                    rhs=cw[:, at : at + width].bitcast(FP8X4),
                    rhs_scale=cs[:, at : at + width],
                    start=True,
                    stop=True,
                )
            relu = ring.tile([N, CH], F32, name="relu")
            for lo, hi, e in spans_of(c):
                nc.scalar.activation(relu[:, lo:hi], bank[:, lo:hi], RELU, bias=b_sb[:, e : e + 1])
            square = ring.tile([N, CH], F32, name="square")
            nc.scalar.activation(square[:], relu[:], SQUARE)
            squares[c] = square

        def scatter(c):
            cols = slice(c * CH, (c + 1) * CH)
            nc.vector.tensor_tensor(
                result[:].indirect(offsets[:, c * CH // 16 : (c + 1) * CH // 16]), squares[c][:], gate_sb[:, cols], MULT
            )

        cast(loads[0], (1280, 2048))
        cast(loads[1], (704, 1024))
        for load in loads[2:4]:
            cast(load, (320, 512))
        for load in loads[4:6]:
            cast(load, (0, 768))
        cast(loads[6], (0, 640))
        cast(loads[7], (0, 288))
        gather(0, 0, 2048)
        gather(0, 2048, 4096)
        cast(loads[8], (160, 384))

        for step in range(NCH + 4):
            if step in (0, 1):
                gather(1, step * CH, (step + 1) * CH)
            if step in (2, 4, 6):
                gather(1, step * CH, (step + 2) * CH)
            if 0 <= step - 1 < NCH:
                lace(step - 1)
            if 0 <= step - 2 < NCH:
                quantise(step - 2)
                multiply(step - 2)
            if 0 <= step - 4 < NCH:
                scatter(step - 4)
        for queue, lo in ((nc.sync, 0), (nc.scalar, 2048)):
            queue.dma_start(out=out[:, lo : lo + 2048], in_=result[:, lo : lo + 2048])
